import numpy as np
import ml_dtypes


def mxq(x, axis, fmt="e4m3"):
    dtype, down = {"e4m3": (ml_dtypes.float8_e4m3fn, 7), "e5m2": (ml_dtypes.float8_e5m2, 14)}[fmt]
    v = np.moveaxis(np.asarray(x, np.float32).astype(ml_dtypes.bfloat16).astype(np.float64), axis, -1)
    blocks = v.reshape(v.shape[:-1] + (-1, 32))
    amax = np.abs(blocks).max(-1, keepdims=True)
    byte = np.maximum(np.where(amax > 0, np.frexp(amax)[1] - 1 + 127, 0) - down, 1)
    scale = np.exp2(byte - 127.0)
    codes = (blocks / scale).astype(np.float32).astype(dtype).astype(np.float64)
    return np.moveaxis((codes * scale).reshape(v.shape), -1, axis)


WIDE = False


def mx_kscale(k):
    if not WIDE:
        return np.ones(k)
    levels = np.array([10, -10, 5, -5, 0])
    if k % 512:
        return np.exp2(np.random.permutation(np.resize(levels, k // 32))).repeat(32)
    a = np.empty((k // 512, 16))
    for p in range(k // 512):
        a[p, :8] = np.random.permutation(np.resize(levels, 8))
        for g in range(8):
            far = levels[np.abs(levels - a[p, g]) >= 10]
            a[p, g + 8] = far[np.random.randint(len(far))]
    return np.exp2(a.ravel()).repeat(32)


def f64(x):
    return np.asarray(x).astype(np.float64)


def striped(idx):
    return np.tile(idx.reshape(-1, 16).T, (8, 1)).astype(np.uint16)


def unstriped(offs):
    return offs[:16].T.reshape(-1).astype(np.int64)


E2M1 = np.array([0.0, 0.5, 1.0, 1.5, 2.0, 3.0, 4.0, 6.0, -0.0, -0.5, -1.0, -1.5, -2.0, -3.0, -4.0, -6.0])


def pack_weight(w, fmt):
    k, n = w.shape
    w = f64(np.asarray(w, np.float32).astype(ml_dtypes.bfloat16)).reshape(k // 32, 32, n)
    amax = np.abs(w).max(1)
    if fmt == "e4m3":
        byte = np.frexp(amax)[1] - 1 + 127 - 7
    else:
        mant, ex = np.frexp(amax / 6.0)
        byte = np.where(mant > 0.5, ex, ex - 1) + 127
    byte = np.clip(np.where(amax > 0, byte, 1), 1, 254)
    scaled = (w * np.exp2(127.0 - byte)[:, None, :]).reshape(k, n).astype(np.float32)
    by_word = np.ascontiguousarray(scaled.reshape(k // 512, 128, 4, n).transpose(0, 1, 3, 2))
    if fmt == "e4m3":
        words = by_word.astype(ml_dtypes.float8_e4m3fn).view(np.uint8)
    else:
        c = by_word.astype(ml_dtypes.float4_e2m1fn).view(np.uint8) & 0xF
        words = (c[..., 0::2] | (c[..., 1::2] << 4)).reshape(k // 512, 128, 2 * n)
    return np.ascontiguousarray(words), np.ascontiguousarray(byte.astype(np.uint8).reshape(k // 512, 16, n))


def unpack_weight(words, scales, fmt):
    g, _, n = scales.shape
    words = np.ascontiguousarray(words).reshape(g, 128, n, -1)
    if fmt == "e4m3":
        vals = words.view(ml_dtypes.float8_e4m3fn).astype(np.float64)
    else:
        nib = np.empty((g, 128, n, 4), np.uint8)
        nib[..., 0::2] = words & 0xF
        nib[..., 1::2] = words >> 4
        vals = E2M1[nib]
    vals = vals * np.repeat(np.exp2(scales.astype(np.float64) - 127.0), 8, axis=1)[..., None]
    return vals.transpose(0, 1, 3, 2).reshape(g * 512, n)


def gelu(v):
    return 0.5 * v * (1.0 + np.tanh(np.sqrt(2.0 / np.pi) * (v + 0.044715 * v**3)))


K, H, T, S, T2, P = 1024, 512, 4096, 1024, 2048, 1024

def setup_inputs():
    n = np.random.standard_normal
    s = mx_kscale(K)[:, None]
    u = mx_kscale(H)[:, None]
    d = {}
    d["tab_words"], d["tab_scales"] = pack_weight(n((K, T)) * s, "e4m3")
    d["offs"] = striped(np.random.permutation(T)[:S])
    d["offs2"] = striped(np.random.permutation(T2)[:S])
    d["offs3"] = striped(np.random.permutation(T2)[:P])
    d["offs4"] = striped(np.random.permutation(T2)[:P])
    d["w1"] = (1.5 * n((K, H)) / s / K ** 0.5).astype(np.float32)
    d["w2_words"], d["w2_scales"] = pack_weight(n((K, H)) / s / K ** 0.5, "e2m1")
    d["wgs"] = np.exp(0.3 * n((128, S))).astype(np.float32)
    d["page0"] = n((H, T2)).astype(np.float32)
    d["sc"] = (np.exp(0.4 * n(H)) * u[:, 0]).astype(np.float32)
    d["w3_words"], d["w3_scales"] = pack_weight(n((H, H)) / u / H ** 0.5, "e4m3")
    d["ng"] = np.exp(0.4 * n(H)).astype(np.float32)
    return d

def reference(tab_words, tab_scales, offs, offs2, offs3, offs4, w1, w2_words, w2_scales,
              wgs, page0, sc, w3_words, w3_scales, ng):
    v = unpack_weight(tab_words, tab_scales, "e4m3")[:, unstriped(offs)]
    w2 = unpack_weight(w2_words, w2_scales, "e2m1")
    w3 = unpack_weight(w3_words, w3_scales, "e4m3")
    a = mxq(f64(w1), 0, "e4m3").T @ v
    b = w2.T @ v
    h = np.maximum(a / (1.0 + np.exp(-a)), b)
    page = f64(page0).copy()
    page[:, unstriped(offs2)] = np.tile(f64(wgs), (H // 128, 1)) * h
    x = page[:, unstriped(offs3)] * f64(sc)[:, None]
    y = w3.T @ mxq(x, 0, "e4m3")
    near = np.tanh(page[:, unstriped(offs4)] * f64(ng)[:, None])
    return y * near + y

@@ -1,0 +1,308 @@
+from contextlib import ExitStack
+
+import concourse.mybir as mybir
+from concourse.masks import make_identity
+
+K, H, T, S, T2, J = 1024, 512, 4096, 1024, 2048, 1024
+FLOPS = 2 * (2 * K * H * S + H * H * J)
+
+F32 = mybir.dt.float32
+BF16 = mybir.dt.bfloat16
+I32 = mybir.dt.int32
+U32 = mybir.dt.uint32
+U16 = mybir.dt.uint16
+U8 = mybir.dt.uint8
+E4M3 = mybir.dt.float8_e4m3fn_x4
+E2M1 = mybir.dt.float4_e2m1fn_x4
+ALU = mybir.AluOpType
+ACT = mybir.ActivationFunctionType
+
+P = 128
+PASSES = 2
+TILES = 4
+N = 512
+LC = N // 16
+
+
+def tile_list_vending_route_scores_kernel(
+    tc, tab_words, tab_scales, offs, offs2, offs3, offs4, w1, w2_words, w2_scales,
+    wgs, page0, sc, w3_words, w3_scales, ng, out,
+):
+    nc = tc.nc
+    with ExitStack() as ctx:
+        pool = ctx.enter_context(tc.tile_pool(name="sb", bufs=1))
+        psum = ctx.enter_context(tc.psum_pool(name="ps", bufs=1))
+
+        def sb(name, shape, dtype, tag=None):
+            return pool.tile(shape, dtype, name=name, tag=tag or name, align_bytes=64)
+
+        def bank(name, tag, shape=None, dtype=F32):
+            return psum.tile(shape or [P, N], dtype, name=name, tag=tag)
+
+        def half(h):
+            return slice(h * N, (h + 1) * N)
+
+        def list_half(tile, h):
+            return tile[:, h * LC:(h + 1) * LC]
+
+        def load_list(name, src):
+            tile = sb(name, [P, S // 16], U16)
+            nc.sync.dma_start(tile[:], src)
+            return tile
+
+        def load_scale_rows(queue, tile, src):
+            for q in range(4):
+                queue.dma_start(
+                    tile[32 * q:32 * q + 4, :].bitcast(I32).rearrange("r (a w) -> r a w", a=src.shape[0]),
+                    src[:, 4 * q:4 * q + 4, :].bitcast(I32).rearrange("a r w -> r a w"),
+                )
+
+        def load_column(name, src):
+            tile = sb(name, [P, TILES], F32)
+            with nc.allow_non_contiguous_dma(reason="one value a partition and row tile"):
+                nc.sync.dma_start(tile[:], src.rearrange("(u p) -> p u", p=P))
+            return tile
+
+        tab_s = sb("tab_s", [P, PASSES * T], U8)
+        nc.gpsimd.memset(tab_s[:, :T].bitcast(I32), 0)
+        nc.vector.memset(tab_s[:, T:].bitcast(I32), 0)
+        w2_s = sb("w2_s", [P, PASSES * H], U8)
+        nc.gpsimd.memset(w2_s[:].bitcast(I32), 0)
+        w3_s = sb("w3_s", [P, H], U8)
+        nc.gpsimd.memset(w3_s[:].bitcast(I32), 0)
+
+        tab_w = [sb("tab_w%d" % a, [P, T], I32) for a in range(PASSES)]
+        tab_src = [tab_words[a].rearrange("p t i -> p (t i)").bitcast(I32) for a in range(PASSES)]
+        w1_rows = w1.rearrange("(a p i) c -> a p i c", a=PASSES, i=4)
+        w1_first = [sb("w1_first%d" % a, [P, 4, P], F32) for a in range(PASSES)]
+        w1_rest = [sb("w1_rest%d" % a, [P, 4, H - P], F32) for a in range(PASSES)]
+        page = [sb("page%d" % u, [P, T2], F32) for u in range(TILES)]
+
+        idx = load_list("idx", offs)
+        idx2 = load_list("idx2", offs2)
+        idx3 = load_list("idx3", offs3)
+        idx4 = load_list("idx4", offs4)
+        for a in range(PASSES):
+            nc.sync.dma_start(w1_first[a][:], w1_rows[a][:, :, :P])
+        nc.sync.dma_start(tab_w[0][:, :T // 2], tab_src[0][:, :T // 2])
+        nc.sync.dma_start(tab_w[0][:, T // 2:], tab_src[0][:, T // 2:])
+        w2_w = sb("w2_w", [P, PASSES * 2 * H], U8)
+        nc.sync.dma_start(
+            w2_w[:].bitcast(I32).rearrange("p (a w) -> p a w", a=PASSES),
+            w2_words.bitcast(I32).rearrange("a p w -> p a w"),
+        )
+        nc.sync.dma_start(tab_w[1][:], tab_src[1])
+        load_scale_rows(nc.scalar, tab_s, tab_scales)
+        load_scale_rows(nc.gpsimd, w2_s, w2_scales)
+        wgs_t = sb("wgs_t", [P, S], F32)
+        nc.sync.dma_start(wgs_t[:, half(0)], wgs[:, half(0)])
+        nc.sync.dma_start(page[0][:], page0[0:P, :])
+        nc.sync.dma_start(wgs_t[:, half(1)], wgs[:, half(1)])
+        for a in range(PASSES):
+            nc.sync.dma_start(w1_rest[a][:], w1_rows[a][:, :, P:])
+        sc_t = load_column("sc_t", sc)
+        ng_t = load_column("ng_t", ng)
+        nc.sync.dma_start(page[1][:], page0[P:2 * P, :])
+        nc.sync.dma_start(page[2][:], page0[2 * P:3 * P, :])
+        nc.sync.dma_start(page[3][:], page0[3 * P:4 * P, :])
+        w3_w = sb("w3_w", [P, H], I32)
+        nc.sync.dma_start(w3_w[:], w3_words[0].rearrange("p c i -> p (c i)").bitcast(I32))
+        load_scale_rows(nc.gpsimd, w3_s, w3_scales)
+
+        ident_bf = sb("ident_bf", [P, P], BF16)
+        make_identity(nc, ident_bf[:])
+        ident_f = sb("ident_f", [P, P], F32)
+        make_identity(nc, ident_f[:])
+
+        v_w, v_s = {}, {}
+
+        def gather_scales(a, h):
+            v_s[a, h] = sb("v_s%d%d" % (a, h), [P, N], U8)
+            nc.vector.tensor_copy(v_s[a, h][:], tab_s[:, a * T:(a + 1) * T].indirect(list_half(idx, h)))
+
+        def gather_words(a, h, tag=None):
+            v_w[a, h] = sb("v_w%d%d" % (a, h), [P, N], U32, tag)
+            nc.vector.tensor_copy(v_w[a, h][:], tab_w[a][:].bitcast(U32).indirect(list_half(idx, h)))
+
+        w1_g, w1_c, w1_s = {}, {}, {}
+
+        def round_w1(u):
+            w1_g[u] = sb("w1_g%d" % u, [P, PASSES * 4 * P], BF16)
+            for a in range(PASSES):
+                raw = w1_first[a][:] if u == 0 else w1_rest[a][:, :, (u - 1) * P:u * P]
+                nc.scalar.copy(
+                    w1_g[u][:, a * 4 * P:(a + 1) * 4 * P].rearrange("p (c n i) -> p c i n", n=4, i=4),
+                    raw.rearrange("p i (c n) -> p c i n", n=4),
+                )
+
+        def quantize_w1(u):
+            w1_c[u] = sb("w1_c%d" % u, [P, PASSES * P], U32)
+            w1_s[u] = sb("w1_s%d" % u, [P, PASSES * P], U8)
+            nc.vector.quantize_mx(out=w1_c[u][:].bitcast(E4M3), scales=w1_s[u][:], in_=w1_g[u][:])
+
+        silu_t, h_t, b_ps = {}, {}, {}
+
+        def products(u, h):
+            if h == 0:
+                silu_t[u] = sb("silu%d" % u, [P, S], F32)
+            a_ps = bank("a_ps%d%d" % (u, h), "pa%d" % h)
+            b_ps[u, h] = bank("b_ps%d%d" % (u, h), "pb%d" % h)
+            for a in range(PASSES):
+                nc.tensor.matmul_mx(
+                    out=a_ps[:], lhsT=w1_c[u][:, a * P:(a + 1) * P].bitcast(E4M3),
+                    lhsT_scale=w1_s[u][:, a * P:(a + 1) * P],
+                    rhs=v_w[a, h][:].bitcast(E4M3), rhs_scale=v_s[a, h][:],
+                    start=(a == 0), stop=(a == PASSES - 1),
+                )
+            for a in range(PASSES):
+                c0 = a * H + u * P
+                nc.tensor.matmul_mx(
+                    out=b_ps[u, h][:], lhsT=w2_w[:, 2 * c0:2 * (c0 + P)].bitcast(E2M1),
+                    lhsT_scale=w2_s[:, c0:c0 + P],
+                    rhs=v_w[a, h][:].bitcast(E4M3), rhs_scale=v_s[a, h][:],
+                    start=(a == 0), stop=(a == PASSES - 1),
+                )
+            nc.scalar.activation(silu_t[u][:, half(h)], a_ps[:], ACT.Silu)
+
+        def larger(u, h):
+            if h == 0:
+                h_t[u] = sb("h%d" % u, [P, S], F32)
+            nc.vector.tensor_tensor(h_t[u][:, half(h)], silu_t[u][:, half(h)], b_ps[u, h][:], ALU.max)
+
+        def scatter(u, h=None):
+            if h is None:
+                nc.vector.tensor_tensor(page[u][:].indirect(idx2[:]), h_t[u][:], wgs_t[:], ALU.mult)
+            else:
+                nc.vector.tensor_tensor(
+                    page[u][:].indirect(list_half(idx2, h)), h_t[u][:, half(h)], wgs_t[:, half(h)], ALU.mult)
+
+        route, xb = {}, {}
+        x_t = [sb("x_t%d" % h, [P, 4, 2, P], F32) for h in range(2)]
+
+        def gather_route(u, tag):
+            whole = sb("route%d" % u, [P, J], F32, tag)
+            nc.vector.tensor_copy(whole[:], page[u][:].indirect(idx3[:]))
+            for h in range(2):
+                route[u, h] = whole[:, half(h)]
+
+        def gather_route_half(u, h):
+            part = sb("route%d%d" % (u, h), [P, N], F32)
+            nc.vector.tensor_copy(part[:], page[u][:].indirect(list_half(idx3, h)))
+            route[u, h] = part[:]
+
+        def turn_route(u):
+            xb[u] = sb("xb%d" % u, [P, J], BF16)
+            for h in range(2):
+                nc.scalar.activation(xb[u][:, half(h)], route[u, h], ACT.Copy, scale=sc_t[:, u:u + 1])
+            for h in range(2):
+                ps = bank("t_ps%d%d" % (u, h), "pt%d" % h, [P, 4, P], BF16)
+                for b in range(4):
+                    j0 = h * N + b * P
+                    nc.tensor.transpose(ps[:, b, :], xb[u][:, j0:j0 + P], ident_bf[:])
+                nc.scalar.copy(
+                    x_t[h][:, :, :, 32 * u:32 * (u + 1)],
+                    ps[:].bitcast(F32).rearrange("p b (q e) -> p b e q", e=2),
+                )
+
+        x_g, x_c, x_s = {}, {}, {}
+
+        def turn_back(h):
+            x_g[h] = sb("x_g%d" % h, [P, 4 * N], BF16)
+            words = x_g[h][:].bitcast(F32)
+            for g in range(2):
+                ps = bank("u_ps%d%d" % (h, g), "pu%d" % g, [P, 2, 2, P], F32)
+                for b in range(2):
+                    for e in range(2):
+                        nc.tensor.transpose(ps[:, b, e, :], x_t[h][:, 2 * g + b, e, :], ident_f[:])
+                nc.scalar.copy(
+                    words[:, g * N:(g + 1) * N].rearrange("p (b j e) -> p b j e", b=2, e=2),
+                    ps[:].rearrange("p b e j -> p b j e"),
+                )
+
+        def quantize_x(h):
+            x_c[h] = sb("x_c%d" % h, [P, N], U32)
+            x_s[h] = sb("x_s%d" % h, [P, N], U8)
+            nc.vector.quantize_mx(out=x_c[h][:].bitcast(E4M3), scales=x_s[h][:], in_=x_g[h][:])
+
+        nearby, near, y_ps = {}, {}, {}
+
+        def gather_nearby(u, tag):
+            nearby[u] = sb("nearby%d" % u, [P, J], F32, tag)
+            nc.vector.tensor_copy(nearby[u][:], page[u][:].indirect(idx4[:]))
+
+        def squash(u, tag):
+            near[u] = sb("near%d" % u, [P, J], F32, tag)
+            nc.scalar.activation(near[u][:], nearby[u][:], ACT.Tanh, scale=ng_t[:, u:u + 1])
+
+        Y_BANKS = (("pa0", "pa1", "pb0", "pb1"), ("pt0", "pt1", "pu0", "pu1"))
+
+        def product_y(h):
+            for u in range(TILES):
+                y_ps[u, h] = bank("y_ps%d%d" % (u, h), Y_BANKS[h][u])
+                nc.tensor.matmul_mx(
+                    out=y_ps[u, h][:], lhsT=w3_w[:, u * P:(u + 1) * P].bitcast(E4M3),
+                    lhsT_scale=w3_s[:, u * P:(u + 1) * P],
+                    rhs=x_c[h][:].bitcast(E4M3), rhs_scale=x_s[h][:],
+                    start=True, stop=True,
+                )
+
+        def finish(u, h):
+            res = sb("res%d%d" % (u, h), [P, N], F32)
+            nc.vector.scalar_tensor_tensor(
+                res[:], near[u][:, half(h)], 1.0, y_ps[u, h][:], ALU.add, ALU.mult)
+            nc.sync.dma_start(out[u * P:(u + 1) * P, half(h)], res[:])
+
+        round_w1(0)
+        quantize_w1(0)
+        gather_words(0, 0)
+        gather_words(0, 1)
+        gather_scales(0, 0)
+        gather_scales(1, 0)
+        gather_scales(0, 1)
+        gather_scales(1, 1)
+        gather_words(1, 0, "tab_s")
+        gather_words(1, 1)
+        products(0, 0)
+        products(0, 1)
+        larger(0, 0)
+        scatter(0, 0)
+        larger(0, 1)
+        scatter(0, 1)
+        for u in range(1, TILES):
+            round_w1(u)
+            quantize_w1(u)
+        products(1, 0)
+        products(1, 1)
+        gather_route(0, "w1_g1")
+        gather_nearby(0, "w1_g2")
+        larger(1, 0)
+        larger(1, 1)
+        turn_route(0)
+        squash(0, "silu1")
+        for u in range(1, TILES - 1):
+            products(u + 1, 0)
+            products(u + 1, 1)
+            scatter(u)
+            larger(u + 1, 0)
+            larger(u + 1, 1)
+            gather_route(u, "silu%d" % (u + 1))
+            turn_route(u)
+        scatter(3)
+        gather_route_half(3, 0)
+        gather_route_half(3, 1)
+        turn_route(3)
+        gather_nearby(1, "route30")
+        gather_nearby(2, "route31")
+        turn_back(0)
+        turn_back(1)
+        quantize_x(0)
+        quantize_x(1)
+        product_y(0)
+        product_y(1)
+        squash(1, "x_t1")
+        squash(2, "x_g0")
+        gather_nearby(3, "x_g1")
+        squash(3, "near3")
+        for u in range(TILES):
+            for h in range(2):
+                finish(u, h)

@@ -22,6 +22,7 @@ PASSES = 2
 TILES = 4
 N = 512
 LC = N // 16
+CLEAR_SPLIT = 5120
 
 
 def tile_list_vending_route_scores_kernel(
@@ -64,8 +65,8 @@ def tile_list_vending_route_scores_kernel(
             return tile
 
         tab_s = sb("tab_s", [P, PASSES * T], U8)
-        nc.gpsimd.memset(tab_s[:, :T].bitcast(I32), 0)
-        nc.vector.memset(tab_s[:, T:].bitcast(I32), 0)
+        nc.gpsimd.memset(tab_s[:, :CLEAR_SPLIT].bitcast(I32), 0)
+        nc.vector.memset(tab_s[:, CLEAR_SPLIT:].bitcast(I32), 0)
         w2_s = sb("w2_s", [P, PASSES * H], U8)
         nc.gpsimd.memset(w2_s[:].bitcast(I32), 0)
         w3_s = sb("w3_s", [P, H], U8)
@@ -78,28 +79,29 @@ def tile_list_vending_route_scores_kernel(
         w1_rest = [sb("w1_rest%d" % a, [P, 4, H - P], F32) for a in range(PASSES)]
         page = [sb("page%d" % u, [P, T2], F32) for u in range(TILES)]
 
+        w2_src = w2_words.bitcast(I32).rearrange("a p w -> p a w")
+        w2_first = sb("w2_first", [P, PASSES, 2 * P], U8)
+        w2_rest = sb("w2_rest", [P, PASSES, 2 * (H - P)], U8)
+
         idx = load_list("idx", offs)
-        idx2 = load_list("idx2", offs2)
-        idx3 = load_list("idx3", offs3)
-        idx4 = load_list("idx4", offs4)
         for a in range(PASSES):
             nc.sync.dma_start(w1_first[a][:], w1_rows[a][:, :, :P])
+        nc.sync.dma_start(w2_first[:].bitcast(I32), w2_src[:, :, :P // 2])
+        load_scale_rows(nc.sync, tab_s, tab_scales)
         nc.sync.dma_start(tab_w[0][:, :T // 2], tab_src[0][:, :T // 2])
         nc.sync.dma_start(tab_w[0][:, T // 2:], tab_src[0][:, T // 2:])
-        w2_w = sb("w2_w", [P, PASSES * 2 * H], U8)
-        nc.sync.dma_start(
-            w2_w[:].bitcast(I32).rearrange("p (a w) -> p a w", a=PASSES),
-            w2_words.bitcast(I32).rearrange("a p w -> p a w"),
-        )
+        load_scale_rows(nc.sync, w2_s, w2_scales)
         nc.sync.dma_start(tab_w[1][:], tab_src[1])
-        load_scale_rows(nc.scalar, tab_s, tab_scales)
-        load_scale_rows(nc.gpsimd, w2_s, w2_scales)
+        idx2 = load_list("idx2", offs2)
         wgs_t = sb("wgs_t", [P, S], F32)
         nc.sync.dma_start(wgs_t[:, half(0)], wgs[:, half(0)])
         nc.sync.dma_start(page[0][:], page0[0:P, :])
         nc.sync.dma_start(wgs_t[:, half(1)], wgs[:, half(1)])
         for a in range(PASSES):
             nc.sync.dma_start(w1_rest[a][:], w1_rows[a][:, :, P:])
+        nc.sync.dma_start(w2_rest[:].bitcast(I32), w2_src[:, :, P // 2:])
+        idx3 = load_list("idx3", offs3)
+        idx4 = load_list("idx4", offs4)
         sc_t = load_column("sc_t", sc)
         ng_t = load_column("ng_t", ng)
         nc.sync.dma_start(page[1][:], page0[P:2 * P, :])
@@ -107,7 +109,7 @@ def tile_list_vending_route_scores_kernel(
         nc.sync.dma_start(page[3][:], page0[3 * P:4 * P, :])
         w3_w = sb("w3_w", [P, H], I32)
         nc.sync.dma_start(w3_w[:], w3_words[0].rearrange("p c i -> p (c i)").bitcast(I32))
-        load_scale_rows(nc.gpsimd, w3_s, w3_scales)
+        load_scale_rows(nc.sync, w3_s, w3_scales)
 
         ident_bf = sb("ident_bf", [P, P], BF16)
         make_identity(nc, ident_bf[:])
@@ -143,8 +145,7 @@ def tile_list_vending_route_scores_kernel(
         silu_t, h_t, b_ps = {}, {}, {}
 
         def products(u, h):
-            if h == 0:
-                silu_t[u] = sb("silu%d" % u, [P, S], F32)
+            silu_t[u, h] = sb("silu%d%d" % (u, h), [P, N], F32)
             a_ps = bank("a_ps%d%d" % (u, h), "pa%d" % h)
             b_ps[u, h] = bank("b_ps%d%d" % (u, h), "pb%d" % h)
             for a in range(PASSES):
@@ -156,18 +157,19 @@ def tile_list_vending_route_scores_kernel(
                 )
             for a in range(PASSES):
                 c0 = a * H + u * P
+                codes = w2_first[:, a, :] if u == 0 else w2_rest[:, a, 2 * P * (u - 1):2 * P * u]
                 nc.tensor.matmul_mx(
-                    out=b_ps[u, h][:], lhsT=w2_w[:, 2 * c0:2 * (c0 + P)].bitcast(E2M1),
+                    out=b_ps[u, h][:], lhsT=codes.bitcast(E2M1),
                     lhsT_scale=w2_s[:, c0:c0 + P],
                     rhs=v_w[a, h][:].bitcast(E4M3), rhs_scale=v_s[a, h][:],
                     start=(a == 0), stop=(a == PASSES - 1),
                 )
-            nc.scalar.activation(silu_t[u][:, half(h)], a_ps[:], ACT.Silu)
+            nc.scalar.activation(silu_t[u, h][:], a_ps[:], ACT.Silu)
 
         def larger(u, h):
             if h == 0:
                 h_t[u] = sb("h%d" % u, [P, S], F32)
-            nc.vector.tensor_tensor(h_t[u][:, half(h)], silu_t[u][:, half(h)], b_ps[u, h][:], ALU.max)
+            nc.vector.tensor_tensor(h_t[u][:, half(h)], silu_t[u, h][:], b_ps[u, h][:], ALU.max)
 
         def scatter(u, h=None):
             if h is None:
@@ -191,7 +193,7 @@ def tile_list_vending_route_scores_kernel(
             route[u, h] = part[:]
 
         def turn_route(u):
-            xb[u] = sb("xb%d" % u, [P, J], BF16)
+            xb[u] = sb("xb%d" % u, [P, J], BF16, "silu%d1" % (u + 1) if u + 1 < TILES else None)
             for h in range(2):
                 nc.scalar.activation(xb[u][:, half(h)], route[u, h], ACT.Copy, scale=sc_t[:, u:u + 1])
             for h in range(2):
@@ -253,14 +255,14 @@ def tile_list_vending_route_scores_kernel(
             nc.sync.dma_start(out[u * P:(u + 1) * P, half(h)], res[:])
 
         round_w1(0)
-        quantize_w1(0)
-        gather_words(0, 0)
-        gather_words(0, 1)
         gather_scales(0, 0)
         gather_scales(1, 0)
+        quantize_w1(0)
+        gather_words(0, 0)
         gather_scales(0, 1)
         gather_scales(1, 1)
-        gather_words(1, 0, "tab_s")
+        gather_words(0, 1)
+        gather_words(1, 0)
         gather_words(1, 1)
         products(0, 0)
         products(0, 1)
@@ -278,14 +280,14 @@ def tile_list_vending_route_scores_kernel(
         larger(1, 0)
         larger(1, 1)
         turn_route(0)
-        squash(0, "silu1")
+        squash(0, "silu10")
         for u in range(1, TILES - 1):
             products(u + 1, 0)
             products(u + 1, 1)
             scatter(u)
             larger(u + 1, 0)
             larger(u + 1, 1)
-            gather_route(u, "silu%d" % (u + 1))
+            gather_route(u, None)
             turn_route(u)
         scatter(3)
         gather_route_half(3, 0)

@@ -22,7 +22,6 @@ PASSES = 2
 TILES = 4
 N = 512
 LC = N // 16
-CLEAR_SPLIT = 5120
 
 
 def tile_list_vending_route_scores_kernel(
@@ -64,50 +63,57 @@ def tile_list_vending_route_scores_kernel(
                 nc.sync.dma_start(tile[:], src.rearrange("(u p) -> p u", p=P))
             return tile
 
-        tab_s = sb("tab_s", [P, PASSES * T], U8)
-        nc.gpsimd.memset(tab_s[:, :CLEAR_SPLIT].bitcast(I32), 0)
-        nc.vector.memset(tab_s[:, CLEAR_SPLIT:].bitcast(I32), 0)
+        tab_s = sb("tab_s", [P, T], U8)
+        nc.vector.memset(tab_s[:].bitcast(I32), 0)
         w2_s = sb("w2_s", [P, PASSES * H], U8)
         nc.gpsimd.memset(w2_s[:].bitcast(I32), 0)
+        v_s = sb("v_s", [P, PASSES * S], U8)
+        nc.gpsimd.memset(v_s[:].bitcast(I32), 0)
+        load_scale_rows(nc.gpsimd, w2_s, w2_scales)
         w3_s = sb("w3_s", [P, H], U8)
         nc.gpsimd.memset(w3_s[:].bitcast(I32), 0)
 
         tab_w = [sb("tab_w%d" % a, [P, T], I32) for a in range(PASSES)]
         tab_src = [tab_words[a].rearrange("p t i -> p (t i)").bitcast(I32) for a in range(PASSES)]
         w1_rows = w1.rearrange("(a p i) c -> a p i c", a=PASSES, i=4)
-        w1_first = [sb("w1_first%d" % a, [P, 4, P], F32) for a in range(PASSES)]
-        w1_rest = [sb("w1_rest%d" % a, [P, 4, H - P], F32) for a in range(PASSES)]
+        w1_raw = {}
+
+        def load_w1(first, last):
+            for a in range(PASSES):
+                tile = sb("w1_raw%d%d" % (first, a), [P, 4, (last - first) * P], F32)
+                nc.sync.dma_start(tile[:], w1_rows[a][:, :, first * P:last * P])
+                for u in range(first, last):
+                    w1_raw[u, a] = tile[:, :, (u - first) * P:(u - first + 1) * P]
+
         page = [sb("page%d" % u, [P, T2], F32) for u in range(TILES)]
 
         w2_src = w2_words.bitcast(I32).rearrange("a p w -> p a w")
         w2_first = sb("w2_first", [P, PASSES, 2 * P], U8)
         w2_rest = sb("w2_rest", [P, PASSES, 2 * (H - P)], U8)
 
+        wgs_t = sb("wgs_t", [P, S], F32)
+        w3_w = sb("w3_w", [P, H], I32)
+
         idx = load_list("idx", offs)
-        for a in range(PASSES):
-            nc.sync.dma_start(w1_first[a][:], w1_rows[a][:, :, :P])
+        load_w1(0, 1)
         nc.sync.dma_start(w2_first[:].bitcast(I32), w2_src[:, :, :P // 2])
-        load_scale_rows(nc.sync, tab_s, tab_scales)
+        nc.sync.dma_start(tab_s[0:P:4, :].bitcast(I32), tab_scales.rearrange("a q t -> (a q) t").bitcast(I32))
         nc.sync.dma_start(tab_w[0][:, :T // 2], tab_src[0][:, :T // 2])
         nc.sync.dma_start(tab_w[0][:, T // 2:], tab_src[0][:, T // 2:])
-        load_scale_rows(nc.sync, w2_s, w2_scales)
         nc.sync.dma_start(tab_w[1][:], tab_src[1])
         idx2 = load_list("idx2", offs2)
-        wgs_t = sb("wgs_t", [P, S], F32)
         nc.sync.dma_start(wgs_t[:, half(0)], wgs[:, half(0)])
         nc.sync.dma_start(page[0][:], page0[0:P, :])
+        load_w1(1, 2)
         nc.sync.dma_start(wgs_t[:, half(1)], wgs[:, half(1)])
-        for a in range(PASSES):
-            nc.sync.dma_start(w1_rest[a][:], w1_rows[a][:, :, P:])
         nc.sync.dma_start(w2_rest[:].bitcast(I32), w2_src[:, :, P // 2:])
+        load_w1(2, TILES)
         idx3 = load_list("idx3", offs3)
-        idx4 = load_list("idx4", offs4)
         sc_t = load_column("sc_t", sc)
+        for u in range(1, TILES):
+            nc.sync.dma_start(page[u][:], page0[u * P:(u + 1) * P, :])
+        idx4 = load_list("idx4", offs4)
         ng_t = load_column("ng_t", ng)
-        nc.sync.dma_start(page[1][:], page0[P:2 * P, :])
-        nc.sync.dma_start(page[2][:], page0[2 * P:3 * P, :])
-        nc.sync.dma_start(page[3][:], page0[3 * P:4 * P, :])
-        w3_w = sb("w3_w", [P, H], I32)
         nc.sync.dma_start(w3_w[:], w3_words[0].rearrange("p c i -> p (c i)").bitcast(I32))
         load_scale_rows(nc.sync, w3_s, w3_scales)
 
@@ -116,11 +122,18 @@ def tile_list_vending_route_scores_kernel(
         ident_f = sb("ident_f", [P, P], F32)
         make_identity(nc, ident_f[:])
 
-        v_w, v_s = {}, {}
+        v_w = {}
 
-        def gather_scales(a, h):
-            v_s[a, h] = sb("v_s%d%d" % (a, h), [P, N], U8)
-            nc.vector.tensor_copy(v_s[a, h][:], tab_s[:, a * T:(a + 1) * T].indirect(list_half(idx, h)))
+        def gather_scales():
+            picked = sb("picked_s", [P, S], U8)
+            nc.vector.tensor_copy(picked[:], tab_s[:].indirect(idx[:]))
+            for a in range(PASSES):
+                for q in range(4):
+                    row = 64 * a + 16 * q
+                    nc.scalar.dma_start(
+                        v_s[32 * q:32 * q + 4, a * S:(a + 1) * S].bitcast(I32),
+                        picked[row:row + 16:4, :].bitcast(I32),
+                    )
 
         def gather_words(a, h, tag=None):
             v_w[a, h] = sb("v_w%d%d" % (a, h), [P, N], U32, tag)
@@ -131,10 +144,9 @@ def tile_list_vending_route_scores_kernel(
         def round_w1(u):
             w1_g[u] = sb("w1_g%d" % u, [P, PASSES * 4 * P], BF16)
             for a in range(PASSES):
-                raw = w1_first[a][:] if u == 0 else w1_rest[a][:, :, (u - 1) * P:u * P]
                 nc.scalar.copy(
                     w1_g[u][:, a * 4 * P:(a + 1) * 4 * P].rearrange("p (c n i) -> p c i n", n=4, i=4),
-                    raw.rearrange("p i (c n) -> p c i n", n=4),
+                    w1_raw[u, a].rearrange("p i (c n) -> p c i n", n=4),
                 )
 
         def quantize_w1(u):
@@ -152,7 +164,7 @@ def tile_list_vending_route_scores_kernel(
                 nc.tensor.matmul_mx(
                     out=a_ps[:], lhsT=w1_c[u][:, a * P:(a + 1) * P].bitcast(E4M3),
                     lhsT_scale=w1_s[u][:, a * P:(a + 1) * P],
-                    rhs=v_w[a, h][:].bitcast(E4M3), rhs_scale=v_s[a, h][:],
+                    rhs=v_w[a, h][:].bitcast(E4M3), rhs_scale=v_s[:, a * S + h * N:a * S + (h + 1) * N],
                     start=(a == 0), stop=(a == PASSES - 1),
                 )
             for a in range(PASSES):
@@ -161,22 +173,26 @@ def tile_list_vending_route_scores_kernel(
                 nc.tensor.matmul_mx(
                     out=b_ps[u, h][:], lhsT=codes.bitcast(E2M1),
                     lhsT_scale=w2_s[:, c0:c0 + P],
-                    rhs=v_w[a, h][:].bitcast(E4M3), rhs_scale=v_s[a, h][:],
+                    rhs=v_w[a, h][:].bitcast(E4M3), rhs_scale=v_s[:, a * S + h * N:a * S + (h + 1) * N],
                     start=(a == 0), stop=(a == PASSES - 1),
                 )
             nc.scalar.activation(silu_t[u, h][:], a_ps[:], ACT.Silu)
 
-        def larger(u, h):
-            if h == 0:
-                h_t[u] = sb("h%d" % u, [P, S], F32)
-            nc.vector.tensor_tensor(h_t[u][:, half(h)], silu_t[u, h][:], b_ps[u, h][:], ALU.max)
+        def larger(u, h, dst):
+            nc.vector.tensor_tensor(dst, silu_t[u, h][:], b_ps[u, h][:], ALU.max)
 
-        def scatter(u, h=None):
-            if h is None:
-                nc.vector.tensor_tensor(page[u][:].indirect(idx2[:]), h_t[u][:], wgs_t[:], ALU.mult)
-            else:
-                nc.vector.tensor_tensor(
-                    page[u][:].indirect(list_half(idx2, h)), h_t[u][:, half(h)], wgs_t[:, half(h)], ALU.mult)
+        def features(u):
+            h_t[u] = sb("h%d" % u, [P, S], F32)
+            for h in range(2):
+                larger(u, h, h_t[u][:, half(h)])
+
+        def scatter(u):
+            nc.vector.tensor_tensor(page[u][:].indirect(idx2[:]), h_t[u][:], wgs_t[:], ALU.mult)
+
+        def first_tile_half(h, tag):
+            part = sb("h0%d" % h, [P, N], F32, tag)
+            larger(0, h, part[:])
+            nc.vector.tensor_tensor(page[0][:].indirect(list_half(idx2, h)), part[:], wgs_t[:, half(h)], ALU.mult)
 
         route, xb = {}, {}
         x_t = [sb("x_t%d" % h, [P, 4, 2, P], F32) for h in range(2)]
@@ -248,63 +264,51 @@ def tile_list_vending_route_scores_kernel(
                     start=True, stop=True,
                 )
 
-        def finish(u, h):
-            res = sb("res%d%d" % (u, h), [P, N], F32)
+        def finish(u, h, res):
             nc.vector.scalar_tensor_tensor(
-                res[:], near[u][:, half(h)], 1.0, y_ps[u, h][:], ALU.add, ALU.mult)
-            nc.sync.dma_start(out[u * P:(u + 1) * P, half(h)], res[:])
+                res, near[u][:, half(h)], 1.0, y_ps[u, h][:], ALU.add, ALU.mult)
+            nc.sync.dma_start(out[u * P:(u + 1) * P, half(h)], res)
 
         round_w1(0)
-        gather_scales(0, 0)
-        gather_scales(1, 0)
+        gather_scales()
         quantize_w1(0)
-        gather_words(0, 0)
-        gather_scales(0, 1)
-        gather_scales(1, 1)
-        gather_words(0, 1)
-        gather_words(1, 0)
-        gather_words(1, 1)
+        for a in range(PASSES):
+            for h in range(2):
+                gather_words(a, h)
         products(0, 0)
         products(0, 1)
-        larger(0, 0)
-        scatter(0, 0)
-        larger(0, 1)
-        scatter(0, 1)
-        for u in range(1, TILES):
+        first_tile_half(0, None)
+        round_w1(1)
+        quantize_w1(1)
+        first_tile_half(1, "w1_g1")
+        for u in range(2, TILES):
             round_w1(u)
             quantize_w1(u)
-        products(1, 0)
-        products(1, 1)
-        gather_route(0, "w1_g1")
-        gather_nearby(0, "w1_g2")
-        larger(1, 0)
-        larger(1, 1)
-        turn_route(0)
-        squash(0, "silu10")
-        for u in range(1, TILES - 1):
-            products(u + 1, 0)
-            products(u + 1, 1)
+        for u in range(1, TILES):
+            products(u, 0)
+            products(u, 1)
+            features(u)
+            gather_route(u - 1, "silu%d0" % u)
+            turn_route(u - 1)
             scatter(u)
-            larger(u + 1, 0)
-            larger(u + 1, 1)
-            gather_route(u, None)
-            turn_route(u)
-        scatter(3)
         gather_route_half(3, 0)
         gather_route_half(3, 1)
         turn_route(3)
-        gather_nearby(1, "route30")
-        gather_nearby(2, "route31")
+        gather_nearby(0, "route30")
+        gather_nearby(1, "route31")
+        gather_nearby(2, "xb3")
         turn_back(0)
         turn_back(1)
         quantize_x(0)
         quantize_x(1)
         product_y(0)
         product_y(1)
-        squash(1, "x_t1")
-        squash(2, "x_g0")
+        squash(0, "x_g0")
+        squash(1, "route30")
+        squash(2, "route31")
         gather_nearby(3, "x_g1")
         squash(3, "near3")
+        res = [sb("res0", [P, TILES * N], F32, "page3"), sb("res1", [P, TILES * N], F32)]
         for u in range(TILES):
             for h in range(2):
-                finish(u, h)
+                finish(u, h, res[h][:, u * N:(u + 1) * N])

@@ -102,10 +102,10 @@ def tile_list_vending_route_scores_kernel(
         nc.sync.dma_start(tab_w[0][:, T // 2:], tab_src[0][:, T // 2:])
         nc.sync.dma_start(tab_w[1][:], tab_src[1])
         idx2 = load_list("idx2", offs2)
-        nc.sync.dma_start(wgs_t[:, half(0)], wgs[:, half(0)])
+        nc.sync.dma_start(wgs_t[:, :N // 2], wgs[:, :N // 2])
         nc.sync.dma_start(page[0][:], page0[0:P, :])
+        nc.sync.dma_start(wgs_t[:, N // 2:], wgs[:, N // 2:])
         load_w1(1, 2)
-        nc.sync.dma_start(wgs_t[:, half(1)], wgs[:, half(1)])
         nc.sync.dma_start(w2_rest[:].bitcast(I32), w2_src[:, :, P // 2:])
         load_w1(2, TILES)
         idx3 = load_list("idx3", offs3)
@@ -156,43 +156,50 @@ def tile_list_vending_route_scores_kernel(
 
         silu_t, h_t, b_ps = {}, {}, {}
 
-        def products(u, h):
-            silu_t[u, h] = sb("silu%d%d" % (u, h), [P, N], F32)
-            a_ps = bank("a_ps%d%d" % (u, h), "pa%d" % h)
-            b_ps[u, h] = bank("b_ps%d%d" % (u, h), "pb%d" % h)
+        def products(u, j0, width, a_tag, b_tag):
+            h, c = divmod(j0, N)
+            key = "%d_%d" % (u, j0)
+            silu_t[u, j0] = sb("silu" + key, [P, width], F32)
+            a_ps = bank("a_ps" + key, a_tag, [P, width])
+            b_ps[u, j0] = bank("b_ps" + key, b_tag, [P, width])
             for a in range(PASSES):
                 nc.tensor.matmul_mx(
                     out=a_ps[:], lhsT=w1_c[u][:, a * P:(a + 1) * P].bitcast(E4M3),
                     lhsT_scale=w1_s[u][:, a * P:(a + 1) * P],
-                    rhs=v_w[a, h][:].bitcast(E4M3), rhs_scale=v_s[:, a * S + h * N:a * S + (h + 1) * N],
+                    rhs=v_w[a, h][:, c:c + width].bitcast(E4M3),
+                    rhs_scale=v_s[:, a * S + j0:a * S + j0 + width],
                     start=(a == 0), stop=(a == PASSES - 1),
                 )
-            for a in range(PASSES):
-                c0 = a * H + u * P
-                codes = w2_first[:, a, :] if u == 0 else w2_rest[:, a, 2 * P * (u - 1):2 * P * u]
-                nc.tensor.matmul_mx(
-                    out=b_ps[u, h][:], lhsT=codes.bitcast(E2M1),
-                    lhsT_scale=w2_s[:, c0:c0 + P],
-                    rhs=v_w[a, h][:].bitcast(E4M3), rhs_scale=v_s[:, a * S + h * N:a * S + (h + 1) * N],
-                    start=(a == 0), stop=(a == PASSES - 1),
-                )
-            nc.scalar.activation(silu_t[u, h][:], a_ps[:], ACT.Silu)
+            step = N if width == N else P
+            for o in range(0, width, step):
+                for a in range(PASSES):
+                    c0 = a * H + u * P
+                    codes = w2_first[:, a, :] if u == 0 else w2_rest[:, a, 2 * P * (u - 1):2 * P * u]
+                    nc.tensor.matmul_mx(
+                        out=b_ps[u, j0][:, o:o + step], lhsT=codes.bitcast(E2M1),
+                        lhsT_scale=w2_s[:, c0:c0 + P],
+                        rhs=v_w[a, h][:, c + o:c + o + step].bitcast(E4M3),
+                        rhs_scale=v_s[:, a * S + j0 + o:a * S + j0 + o + step],
+                        start=(a == 0), stop=(a == PASSES - 1),
+                    )
+            nc.scalar.activation(silu_t[u, j0][:], a_ps[:], ACT.Silu)
 
-        def larger(u, h, dst):
-            nc.vector.tensor_tensor(dst, silu_t[u, h][:], b_ps[u, h][:], ALU.max)
+        def larger(u, j0, dst):
+            nc.vector.tensor_tensor(dst, silu_t[u, j0][:], b_ps[u, j0][:], ALU.max)
 
         def features(u):
             h_t[u] = sb("h%d" % u, [P, S], F32)
             for h in range(2):
-                larger(u, h, h_t[u][:, half(h)])
+                larger(u, h * N, h_t[u][:, half(h)])
 
         def scatter(u):
             nc.vector.tensor_tensor(page[u][:].indirect(idx2[:]), h_t[u][:], wgs_t[:], ALU.mult)
 
-        def first_tile_half(h, tag):
-            part = sb("h0%d" % h, [P, N], F32, tag)
-            larger(0, h, part[:])
-            nc.vector.tensor_tensor(page[0][:].indirect(list_half(idx2, h)), part[:], wgs_t[:, half(h)], ALU.mult)
+        def first_tile_part(j0, width, tag):
+            part = sb("h0_%d" % j0, [P, width], F32, tag)
+            larger(0, j0, part[:])
+            nc.vector.tensor_tensor(
+                page[0][:].indirect(idx2[:, j0 // 16:(j0 + width) // 16]), part[:], wgs_t[:, j0:j0 + width], ALU.mult)
 
         route, xb = {}, {}
         x_t = [sb("x_t%d" % h, [P, 4, 2, P], F32) for h in range(2)]
@@ -209,7 +216,7 @@ def tile_list_vending_route_scores_kernel(
             route[u, h] = part[:]
 
         def turn_route(u):
-            xb[u] = sb("xb%d" % u, [P, J], BF16, "silu%d1" % (u + 1) if u + 1 < TILES else None)
+            xb[u] = sb("xb%d" % u, [P, J], BF16, "silu%d_%d" % (u + 1, N) if u + 1 < TILES else None)
             for h in range(2):
                 nc.scalar.activation(xb[u][:, half(h)], route[u, h], ACT.Copy, scale=sc_t[:, u:u + 1])
             for h in range(2):
@@ -243,6 +250,8 @@ def tile_list_vending_route_scores_kernel(
             nc.vector.quantize_mx(out=x_c[h][:].bitcast(E4M3), scales=x_s[h][:], in_=x_g[h][:])
 
         nearby, near, y_ps = {}, {}, {}
+        ng2_t = sb("ng2_t", [P, TILES], F32)
+        nc.scalar.activation(ng2_t[:], ng_t[:], ACT.Copy, scale=2.0)
 
         def gather_nearby(u, tag):
             nearby[u] = sb("nearby%d" % u, [P, J], F32, tag)
@@ -250,7 +259,7 @@ def tile_list_vending_route_scores_kernel(
 
         def squash(u, tag):
             near[u] = sb("near%d" % u, [P, J], F32, tag)
-            nc.scalar.activation(near[u][:], nearby[u][:], ACT.Tanh, scale=ng_t[:, u:u + 1])
+            nc.scalar.activation(near[u][:], nearby[u][:], ACT.Sigmoid, scale=ng2_t[:, u:u + 1])
 
         Y_BANKS = (("pa0", "pa1", "pb0", "pb1"), ("pt0", "pt1", "pu0", "pu1"))
 
@@ -266,8 +275,15 @@ def tile_list_vending_route_scores_kernel(
 
         def finish(u, h, res):
             nc.vector.scalar_tensor_tensor(
-                res, near[u][:, half(h)], 1.0, y_ps[u, h][:], ALU.add, ALU.mult)
+                res, near[u][:, half(h)], 2.0, y_ps[u, h][:], ALU.mult, ALU.mult)
             nc.sync.dma_start(out[u * P:(u + 1) * P, half(h)], res)
+
+        def finish_on_gpsimd(u, h):
+            y2 = sb("y2_%d%d" % (u, h), [P, N], F32)
+            nc.scalar.activation(y2[:], y_ps[u, h][:], ACT.Copy, scale=2.0)
+            res = sb("res_g%d%d" % (u, h), [P, N], F32)
+            nc.gpsimd.tensor_tensor(res[:], y2[:], near[u][:, half(h)], ALU.mult)
+            nc.sync.dma_start(out[u * P:(u + 1) * P, half(h)], res[:])
 
         round_w1(0)
         gather_scales()
@@ -275,20 +291,22 @@ def tile_list_vending_route_scores_kernel(
         for a in range(PASSES):
             for h in range(2):
                 gather_words(a, h)
-        products(0, 0)
-        products(0, 1)
-        first_tile_half(0, None)
+        products(0, 0, N // 2, "pt0", "pt1")
+        products(0, N // 2, N // 2, "pa0", "pb0")
+        products(0, N, N, "pa1", "pb1")
+        first_tile_part(0, N // 2, None)
+        first_tile_part(N // 2, N // 2, None)
         round_w1(1)
         quantize_w1(1)
-        first_tile_half(1, "w1_g1")
+        first_tile_part(N, N, "w1_g1")
         for u in range(2, TILES):
             round_w1(u)
             quantize_w1(u)
         for u in range(1, TILES):
-            products(u, 0)
-            products(u, 1)
+            for h in range(2):
+                products(u, h * N, N, "pa%d" % h, "pb%d" % h)
             features(u)
-            gather_route(u - 1, "silu%d0" % u)
+            gather_route(u - 1, "silu%d_0" % u)
             turn_route(u - 1)
             scatter(u)
         gather_route_half(3, 0)
@@ -303,12 +321,14 @@ def tile_list_vending_route_scores_kernel(
         quantize_x(1)
         product_y(0)
         product_y(1)
-        squash(0, "x_g0")
+        squash(0, "x_t1")
         squash(1, "route30")
         squash(2, "route31")
+        for u in range(TILES - 1):
+            finish_on_gpsimd(u, 0)
         gather_nearby(3, "x_g1")
         squash(3, "near3")
-        res = [sb("res0", [P, TILES * N], F32, "page3"), sb("res1", [P, TILES * N], F32)]
+        res = sb("res", [P, (TILES + 1) * N], F32)
         for u in range(TILES):
-            for h in range(2):
-                finish(u, h, res[h][:, u * N:(u + 1) * N])
+            finish(u, 1, res[:, u * N:(u + 1) * N])
+        finish(TILES - 1, 0, res[:, TILES * N:])

@@ -187,13 +187,29 @@ def tile_list_vending_route_scores_kernel(
         def larger(u, j0, dst):
             nc.vector.tensor_tensor(dst, silu_t[u, j0][:], b_ps[u, j0][:], ALU.max)
 
-        def features(u):
+        def features_on_vector(u):
             h_t[u] = sb("h%d" % u, [P, S], F32)
             for h in range(2):
                 larger(u, h * N, h_t[u][:, half(h)])
+            for h in range(2):
+                nc.gpsimd.tensor_tensor(h_t[u][:, half(h)], h_t[u][:, half(h)], wgs_t[:, half(h)], ALU.mult)
+
+        def features_on_gpsimd(u):
+            h_t[u] = sb("h%d" % u, [P, S], F32)
+            b_sb = {}
+            gap = sb("gap%d" % u, [P, S], F32, "gap")
+            for h in range(2):
+                b_sb[h] = sb("b_sb%d%d" % (u, h), [P, N], F32)
+                nc.scalar.copy(b_sb[h][:], b_ps[u, h * N][:])
+            for h in range(2):
+                nc.gpsimd.tensor_tensor(gap[:, half(h)], silu_t[u, h * N][:], b_sb[h][:], ALU.subtract)
+                nc.scalar.activation(gap[:, half(h)], gap[:, half(h)], ACT.Relu)
+            for h in range(2):
+                nc.gpsimd.tensor_tensor(gap[:, half(h)], gap[:, half(h)], b_sb[h][:], ALU.add)
+            nc.gpsimd.tensor_tensor(h_t[u][:], gap[:], wgs_t[:], ALU.mult)
 
         def scatter(u):
-            nc.vector.tensor_tensor(page[u][:].indirect(idx2[:]), h_t[u][:], wgs_t[:], ALU.mult)
+            nc.vector.tensor_copy(page[u][:].indirect(idx2[:]), h_t[u][:])
 
         def first_tile_part(j0, width, tag):
             part = sb("h0_%d" % j0, [P, width], F32, tag)
@@ -215,8 +231,8 @@ def tile_list_vending_route_scores_kernel(
             nc.vector.tensor_copy(part[:], page[u][:].indirect(list_half(idx3, h)))
             route[u, h] = part[:]
 
-        def turn_route(u):
-            xb[u] = sb("xb%d" % u, [P, J], BF16, "silu%d_%d" % (u + 1, N) if u + 1 < TILES else None)
+        def turn_route(u, tag):
+            xb[u] = sb("xb%d" % u, [P, J], BF16, tag)
             for h in range(2):
                 nc.scalar.activation(xb[u][:, half(h)], route[u, h], ACT.Copy, scale=sc_t[:, u:u + 1])
             for h in range(2):
@@ -302,16 +318,23 @@ def tile_list_vending_route_scores_kernel(
         for u in range(2, TILES):
             round_w1(u)
             quantize_w1(u)
-        for u in range(1, TILES):
+        for h in range(2):
+            products(1, h * N, N, "pa%d" % h, "pb%d" % h)
+        features_on_vector(1)
+        gather_route(0, "silu1_%d" % N)
+        for u in range(2, TILES):
             for h in range(2):
                 products(u, h * N, N, "pa%d" % h, "pb%d" % h)
-            features(u)
-            gather_route(u - 1, "silu%d_0" % u)
-            turn_route(u - 1)
-            scatter(u)
+            features_on_gpsimd(u)
+            scatter(u - 1)
+            gather_route(u - 1, None)
+        turn_route(0, "b_sb21")
+        turn_route(1, "b_sb31")
+        turn_route(2, "b_sb30")
+        scatter(3)
         gather_route_half(3, 0)
         gather_route_half(3, 1)
-        turn_route(3)
+        turn_route(3, None)
         gather_nearby(0, "route30")
         gather_nearby(1, "route31")
         gather_nearby(2, "xb3")

from contextlib import ExitStack

import concourse.mybir as mybir
from concourse.masks import make_identity

K, H, T, S, T2, J = 1024, 512, 4096, 1024, 2048, 1024
FLOPS = 2 * (2 * K * H * S + H * H * J)

F32 = mybir.dt.float32
BF16 = mybir.dt.bfloat16
I32 = mybir.dt.int32
U32 = mybir.dt.uint32
U16 = mybir.dt.uint16
U8 = mybir.dt.uint8
E4M3 = mybir.dt.float8_e4m3fn_x4
E2M1 = mybir.dt.float4_e2m1fn_x4
ALU = mybir.AluOpType
ACT = mybir.ActivationFunctionType

P = 128
PASSES = 2
TILES = 4
N = 512
LC = N // 16


def tile_list_vending_route_scores_kernel(
    tc, tab_words, tab_scales, offs, offs2, offs3, offs4, w1, w2_words, w2_scales,
    wgs, page0, sc, w3_words, w3_scales, ng, out,
):
    nc = tc.nc
    with ExitStack() as ctx:
        pool = ctx.enter_context(tc.tile_pool(name="sb", bufs=1))
        psum = ctx.enter_context(tc.psum_pool(name="ps", bufs=1))

        def sb(name, shape, dtype, tag=None):
            return pool.tile(shape, dtype, name=name, tag=tag or name, align_bytes=64)

        def bank(name, tag, shape=None, dtype=F32):
            return psum.tile(shape or [P, N], dtype, name=name, tag=tag)

        def half(h):
            return slice(h * N, (h + 1) * N)

        def list_half(tile, h):
            return tile[:, h * LC:(h + 1) * LC]

        def load_list(name, src):
            tile = sb(name, [P, S // 16], U16)
            nc.sync.dma_start(tile[:], src)
            return tile

        def load_scale_rows(queue, tile, src):
            for q in range(4):
                queue.dma_start(
                    tile[32 * q:32 * q + 4, :].bitcast(I32).rearrange("r (a w) -> r a w", a=src.shape[0]),
                    src[:, 4 * q:4 * q + 4, :].bitcast(I32).rearrange("a r w -> r a w"),
                )

        def load_column(name, src):
            tile = sb(name, [P, TILES], F32)
            with nc.allow_non_contiguous_dma(reason="one value a partition and row tile"):
                nc.sync.dma_start(tile[:], src.rearrange("(u p) -> p u", p=P))
            return tile

        tab_s = sb("tab_s", [P, T], U8)
        nc.vector.memset(tab_s[:].bitcast(I32), 0)
        w2_s = sb("w2_s", [P, PASSES * H], U8)
        nc.gpsimd.memset(w2_s[:].bitcast(I32), 0)
        v_s = sb("v_s", [P, PASSES * S], U8)
        nc.gpsimd.memset(v_s[:].bitcast(I32), 0)
        load_scale_rows(nc.gpsimd, w2_s, w2_scales)
        w3_s = sb("w3_s", [P, H], U8)
        nc.gpsimd.memset(w3_s[:].bitcast(I32), 0)

        tab_w = [sb("tab_w%d" % a, [P, T], I32) for a in range(PASSES)]
        tab_src = [tab_words[a].rearrange("p t i -> p (t i)").bitcast(I32) for a in range(PASSES)]
        w1_rows = w1.rearrange("(a p i) c -> a p i c", a=PASSES, i=4)
        w1_raw = {}

        def load_w1(first, last):
            for a in range(PASSES):
                tile = sb("w1_raw%d%d" % (first, a), [P, 4, (last - first) * P], F32)
                nc.sync.dma_start(tile[:], w1_rows[a][:, :, first * P:last * P])
                for u in range(first, last):
                    w1_raw[u, a] = tile[:, :, (u - first) * P:(u - first + 1) * P]

        page = [sb("page%d" % u, [P, T2], F32) for u in range(TILES)]

        w2_src = w2_words.bitcast(I32).rearrange("a p w -> p a w")
        w2_first = sb("w2_first", [P, PASSES, 2 * P], U8)
        w2_rest = sb("w2_rest", [P, PASSES, 2 * (H - P)], U8)

        wgs_t = sb("wgs_t", [P, S], F32)
        w3_w = sb("w3_w", [P, H], I32)

        idx = load_list("idx", offs)
        load_w1(0, 1)
        nc.sync.dma_start(w2_first[:].bitcast(I32), w2_src[:, :, :P // 2])
        nc.sync.dma_start(tab_s[0:P:4, :].bitcast(I32), tab_scales.rearrange("a q t -> (a q) t").bitcast(I32))
        nc.sync.dma_start(tab_w[0][:, :T // 2], tab_src[0][:, :T // 2])
        nc.sync.dma_start(tab_w[0][:, T // 2:], tab_src[0][:, T // 2:])
        nc.sync.dma_start(tab_w[1][:], tab_src[1])
        idx2 = load_list("idx2", offs2)
        nc.sync.dma_start(wgs_t[:, :N // 2], wgs[:, :N // 2])
        nc.sync.dma_start(page[0][:], page0[0:P, :])
        nc.sync.dma_start(wgs_t[:, N // 2:], wgs[:, N // 2:])
        load_w1(1, 2)
        nc.sync.dma_start(w2_rest[:].bitcast(I32), w2_src[:, :, P // 2:])
        load_w1(2, TILES)
        idx3 = load_list("idx3", offs3)
        sc_t = load_column("sc_t", sc)
        for u in range(1, TILES):
            nc.sync.dma_start(page[u][:], page0[u * P:(u + 1) * P, :])
        idx4 = load_list("idx4", offs4)
        ng_t = load_column("ng_t", ng)
        nc.sync.dma_start(w3_w[:], w3_words[0].rearrange("p c i -> p (c i)").bitcast(I32))
        load_scale_rows(nc.sync, w3_s, w3_scales)

        ident_bf = sb("ident_bf", [P, P], BF16)
        make_identity(nc, ident_bf[:])
        ident_f = sb("ident_f", [P, P], F32)
        make_identity(nc, ident_f[:])

        v_w = {}

        def gather_scales():
            picked = sb("picked_s", [P, S], U8)
            nc.vector.tensor_copy(picked[:], tab_s[:].indirect(idx[:]))
            for a in range(PASSES):
                for q in range(4):
                    row = 64 * a + 16 * q
                    nc.scalar.dma_start(
                        v_s[32 * q:32 * q + 4, a * S:(a + 1) * S].bitcast(I32),
                        picked[row:row + 16:4, :].bitcast(I32),
                    )

        def gather_words(a, h, tag=None):
            v_w[a, h] = sb("v_w%d%d" % (a, h), [P, N], U32, tag)
            nc.vector.tensor_copy(v_w[a, h][:], tab_w[a][:].bitcast(U32).indirect(list_half(idx, h)))

        w1_g, w1_c, w1_s = {}, {}, {}

        def round_w1(u):
            w1_g[u] = sb("w1_g%d" % u, [P, PASSES * 4 * P], BF16)
            for a in range(PASSES):
                nc.scalar.copy(
                    w1_g[u][:, a * 4 * P:(a + 1) * 4 * P].rearrange("p (c n i) -> p c i n", n=4, i=4),
                    w1_raw[u, a].rearrange("p i (c n) -> p c i n", n=4),
                )

        def quantize_w1(u):
            w1_c[u] = sb("w1_c%d" % u, [P, PASSES * P], U32)
            w1_s[u] = sb("w1_s%d" % u, [P, PASSES * P], U8)
            nc.vector.quantize_mx(out=w1_c[u][:].bitcast(E4M3), scales=w1_s[u][:], in_=w1_g[u][:])

        silu_t, h_t, b_ps = {}, {}, {}

        def products(u, j0, width, a_tag, b_tag):
            h, c = divmod(j0, N)
            key = "%d_%d" % (u, j0)
            silu_t[u, j0] = sb("silu" + key, [P, width], F32)
            a_ps = bank("a_ps" + key, a_tag, [P, width])
            b_ps[u, j0] = bank("b_ps" + key, b_tag, [P, width])
            for a in range(PASSES):
                nc.tensor.matmul_mx(
                    out=a_ps[:], lhsT=w1_c[u][:, a * P:(a + 1) * P].bitcast(E4M3),
                    lhsT_scale=w1_s[u][:, a * P:(a + 1) * P],
                    rhs=v_w[a, h][:, c:c + width].bitcast(E4M3),
                    rhs_scale=v_s[:, a * S + j0:a * S + j0 + width],
                    start=(a == 0), stop=(a == PASSES - 1),
                )
            step = N if width == N else P
            for o in range(0, width, step):
                for a in range(PASSES):
                    c0 = a * H + u * P
                    codes = w2_first[:, a, :] if u == 0 else w2_rest[:, a, 2 * P * (u - 1):2 * P * u]
                    nc.tensor.matmul_mx(
                        out=b_ps[u, j0][:, o:o + step], lhsT=codes.bitcast(E2M1),
                        lhsT_scale=w2_s[:, c0:c0 + P],
                        rhs=v_w[a, h][:, c + o:c + o + step].bitcast(E4M3),
                        rhs_scale=v_s[:, a * S + j0 + o:a * S + j0 + o + step],
                        start=(a == 0), stop=(a == PASSES - 1),
                    )
            nc.scalar.activation(silu_t[u, j0][:], a_ps[:], ACT.Silu)

        def larger(u, j0, dst):
            nc.vector.tensor_tensor(dst, silu_t[u, j0][:], b_ps[u, j0][:], ALU.max)

        def features_on_vector(u):
            h_t[u] = sb("h%d" % u, [P, S], F32)
            for h in range(2):
                larger(u, h * N, h_t[u][:, half(h)])
            for h in range(2):
                nc.gpsimd.tensor_tensor(h_t[u][:, half(h)], h_t[u][:, half(h)], wgs_t[:, half(h)], ALU.mult)

        def features_on_gpsimd(u):
            h_t[u] = sb("h%d" % u, [P, S], F32)
            b_sb = {}
            gap = sb("gap%d" % u, [P, S], F32, "gap")
            for h in range(2):
                b_sb[h] = sb("b_sb%d%d" % (u, h), [P, N], F32)
                nc.scalar.copy(b_sb[h][:], b_ps[u, h * N][:])
            for h in range(2):
                nc.gpsimd.tensor_tensor(gap[:, half(h)], silu_t[u, h * N][:], b_sb[h][:], ALU.subtract)
                nc.scalar.activation(gap[:, half(h)], gap[:, half(h)], ACT.Relu)
            for h in range(2):
                nc.gpsimd.tensor_tensor(gap[:, half(h)], gap[:, half(h)], b_sb[h][:], ALU.add)
            nc.gpsimd.tensor_tensor(h_t[u][:], gap[:], wgs_t[:], ALU.mult)

        def scatter(u):
            nc.vector.tensor_copy(page[u][:].indirect(idx2[:]), h_t[u][:])

        def first_tile_part(j0, width, tag):
            part = sb("h0_%d" % j0, [P, width], F32, tag)
            larger(0, j0, part[:])
            nc.vector.tensor_tensor(
                page[0][:].indirect(idx2[:, j0 // 16:(j0 + width) // 16]), part[:], wgs_t[:, j0:j0 + width], ALU.mult)

        route, xb = {}, {}
        x_t = [sb("x_t%d" % h, [P, 4, 2, P], F32) for h in range(2)]

        def gather_route(u, tag):
            whole = sb("route%d" % u, [P, J], F32, tag)
            nc.vector.tensor_copy(whole[:], page[u][:].indirect(idx3[:]))
            for h in range(2):
                route[u, h] = whole[:, half(h)]

        def gather_route_half(u, h):
            part = sb("route%d%d" % (u, h), [P, N], F32)
            nc.vector.tensor_copy(part[:], page[u][:].indirect(list_half(idx3, h)))
            route[u, h] = part[:]

        def turn_route(u, tag):
            xb[u] = sb("xb%d" % u, [P, J], BF16, tag)
            for h in range(2):
                nc.scalar.activation(xb[u][:, half(h)], route[u, h], ACT.Copy, scale=sc_t[:, u:u + 1])
            for h in range(2):
                ps = bank("t_ps%d%d" % (u, h), "pt%d" % h, [P, 4, P], BF16)
                for b in range(4):
                    j0 = h * N + b * P
                    nc.tensor.transpose(ps[:, b, :], xb[u][:, j0:j0 + P], ident_bf[:])
                nc.scalar.copy(
                    x_t[h][:, :, :, 32 * u:32 * (u + 1)],
                    ps[:].bitcast(F32).rearrange("p b (q e) -> p b e q", e=2),
                )

        x_g, x_c, x_s = {}, {}, {}

        def turn_back(h):
            x_g[h] = sb("x_g%d" % h, [P, 4 * N], BF16)
            words = x_g[h][:].bitcast(F32)
            for g in range(2):
                ps = bank("u_ps%d%d" % (h, g), "pu%d" % g, [P, 2, 2, P], F32)
                for b in range(2):
                    for e in range(2):
                        nc.tensor.transpose(ps[:, b, e, :], x_t[h][:, 2 * g + b, e, :], ident_f[:])
                nc.scalar.copy(
                    words[:, g * N:(g + 1) * N].rearrange("p (b j e) -> p b j e", b=2, e=2),
                    ps[:].rearrange("p b e j -> p b j e"),
                )

        def quantize_x(h):
            x_c[h] = sb("x_c%d" % h, [P, N], U32)
            x_s[h] = sb("x_s%d" % h, [P, N], U8)
            nc.vector.quantize_mx(out=x_c[h][:].bitcast(E4M3), scales=x_s[h][:], in_=x_g[h][:])

        nearby, near, y_ps = {}, {}, {}
        ng2_t = sb("ng2_t", [P, TILES], F32)
        nc.scalar.activation(ng2_t[:], ng_t[:], ACT.Copy, scale=2.0)

        def gather_nearby(u, tag):
            nearby[u] = sb("nearby%d" % u, [P, J], F32, tag)
            nc.vector.tensor_copy(nearby[u][:], page[u][:].indirect(idx4[:]))

        def squash(u, tag):
            near[u] = sb("near%d" % u, [P, J], F32, tag)
            nc.scalar.activation(near[u][:], nearby[u][:], ACT.Sigmoid, scale=ng2_t[:, u:u + 1])

        Y_BANKS = (("pa0", "pa1", "pb0", "pb1"), ("pt0", "pt1", "pu0", "pu1"))

        def product_y(h):
            for u in range(TILES):
                y_ps[u, h] = bank("y_ps%d%d" % (u, h), Y_BANKS[h][u])
                nc.tensor.matmul_mx(
                    out=y_ps[u, h][:], lhsT=w3_w[:, u * P:(u + 1) * P].bitcast(E4M3),
                    lhsT_scale=w3_s[:, u * P:(u + 1) * P],
                    rhs=x_c[h][:].bitcast(E4M3), rhs_scale=x_s[h][:],
                    start=True, stop=True,
                )

        def finish(u, h, res):
            nc.vector.scalar_tensor_tensor(
                res, near[u][:, half(h)], 2.0, y_ps[u, h][:], ALU.mult, ALU.mult)
            nc.sync.dma_start(out[u * P:(u + 1) * P, half(h)], res)

        def finish_on_gpsimd(u, h):
            y2 = sb("y2_%d%d" % (u, h), [P, N], F32)
            nc.scalar.activation(y2[:], y_ps[u, h][:], ACT.Copy, scale=2.0)
            res = sb("res_g%d%d" % (u, h), [P, N], F32)
            nc.gpsimd.tensor_tensor(res[:], y2[:], near[u][:, half(h)], ALU.mult)
            nc.sync.dma_start(out[u * P:(u + 1) * P, half(h)], res[:])

        round_w1(0)
        gather_scales()
        quantize_w1(0)
        for a in range(PASSES):
            for h in range(2):
                gather_words(a, h)
        products(0, 0, N // 2, "pt0", "pt1")
        products(0, N // 2, N // 2, "pa0", "pb0")
        products(0, N, N, "pa1", "pb1")
        first_tile_part(0, N // 2, None)
        first_tile_part(N // 2, N // 2, None)
        round_w1(1)
        quantize_w1(1)
        first_tile_part(N, N, "w1_g1")
        for u in range(2, TILES):
            round_w1(u)
            quantize_w1(u)
        for h in range(2):
            products(1, h * N, N, "pa%d" % h, "pb%d" % h)
        features_on_vector(1)
        gather_route(0, "silu1_%d" % N)
        for u in range(2, TILES):
            for h in range(2):
                products(u, h * N, N, "pa%d" % h, "pb%d" % h)
            features_on_gpsimd(u)
            scatter(u - 1)
            gather_route(u - 1, None)
        turn_route(0, "b_sb21")
        turn_route(1, "b_sb31")
        turn_route(2, "b_sb30")
        scatter(3)
        gather_route_half(3, 0)
        gather_route_half(3, 1)
        turn_route(3, None)
        gather_nearby(0, "route30")
        gather_nearby(1, "route31")
        gather_nearby(2, "xb3")
        turn_back(0)
        turn_back(1)
        quantize_x(0)
        quantize_x(1)
        product_y(0)
        product_y(1)
        squash(0, "x_t1")
        squash(1, "route30")
        squash(2, "route31")
        for u in range(TILES - 1):
            finish_on_gpsimd(u, 0)
        gather_nearby(3, "x_g1")
        squash(3, "near3")
        res = sb("res", [P, (TILES + 1) * N], F32)
        for u in range(TILES):
            finish(u, 1, res[:, u * N:(u + 1) * N])
        finish(TILES - 1, 0, res[:, TILES * N:])
